import numpy as np
import ml_dtypes


def mxq(x, axis, fmt="e4m3"):
    dtype, down = {"e4m3": (ml_dtypes.float8_e4m3fn, 7), "e5m2": (ml_dtypes.float8_e5m2, 14)}[fmt]
    v = np.moveaxis(np.asarray(x, np.float32).astype(ml_dtypes.bfloat16).astype(np.float64), axis, -1)
    blocks = v.reshape(v.shape[:-1] + (-1, 32))
    amax = np.abs(blocks).max(-1, keepdims=True)
    byte = np.maximum(np.where(amax > 0, np.frexp(amax)[1] - 1 + 127, 0) - down, 1)
    scale = np.exp2(byte - 127.0)
    codes = (blocks / scale).astype(np.float32).astype(dtype).astype(np.float64)
    return np.moveaxis((codes * scale).reshape(v.shape), -1, axis)


WIDE = False


def mx_kscale(k):
    if not WIDE:
        return np.ones(k)
    levels = np.array([10, -10, 5, -5, 0])
    if k % 512:
        return np.exp2(np.random.permutation(np.resize(levels, k // 32))).repeat(32)
    a = np.empty((k // 512, 16))
    for p in range(k // 512):
        a[p, :8] = np.random.permutation(np.resize(levels, 8))
        for g in range(8):
            far = levels[np.abs(levels - a[p, g]) >= 10]
            a[p, g + 8] = far[np.random.randint(len(far))]
    return np.exp2(a.ravel()).repeat(32)


def f64(x):
    return np.asarray(x).astype(np.float64)


def striped(idx):
    return np.tile(idx.reshape(-1, 16).T, (8, 1)).astype(np.uint16)


def unstriped(offs):
    return offs[:16].T.reshape(-1).astype(np.int64)


E2M1 = np.array([0.0, 0.5, 1.0, 1.5, 2.0, 3.0, 4.0, 6.0, -0.0, -0.5, -1.0, -1.5, -2.0, -3.0, -4.0, -6.0])


def pack_weight(w, fmt):
    k, n = w.shape
    w = f64(np.asarray(w, np.float32).astype(ml_dtypes.bfloat16)).reshape(k // 32, 32, n)
    amax = np.abs(w).max(1)
    if fmt == "e4m3":
        byte = np.frexp(amax)[1] - 1 + 127 - 7
    else:
        mant, ex = np.frexp(amax / 6.0)
        byte = np.where(mant > 0.5, ex, ex - 1) + 127
    byte = np.clip(np.where(amax > 0, byte, 1), 1, 254)
    scaled = (w * np.exp2(127.0 - byte)[:, None, :]).reshape(k, n).astype(np.float32)
    by_word = np.ascontiguousarray(scaled.reshape(k // 512, 128, 4, n).transpose(0, 1, 3, 2))
    if fmt == "e4m3":
        words = by_word.astype(ml_dtypes.float8_e4m3fn).view(np.uint8)
    else:
        c = by_word.astype(ml_dtypes.float4_e2m1fn).view(np.uint8) & 0xF
        words = (c[..., 0::2] | (c[..., 1::2] << 4)).reshape(k // 512, 128, 2 * n)
    return np.ascontiguousarray(words), np.ascontiguousarray(byte.astype(np.uint8).reshape(k // 512, 16, n))


def unpack_weight(words, scales, fmt):
    g, _, n = scales.shape
    words = np.ascontiguousarray(words).reshape(g, 128, n, -1)
    if fmt == "e4m3":
        vals = words.view(ml_dtypes.float8_e4m3fn).astype(np.float64)
    else:
        nib = np.empty((g, 128, n, 4), np.uint8)
        nib[..., 0::2] = words & 0xF
        nib[..., 1::2] = words >> 4
        vals = E2M1[nib]
    vals = vals * np.repeat(np.exp2(scales.astype(np.float64) - 127.0), 8, axis=1)[..., None]
    return vals.transpose(0, 1, 3, 2).reshape(g * 512, n)


def gelu(v):
    return 0.5 * v * (1.0 + np.tanh(np.sqrt(2.0 / np.pi) * (v + 0.044715 * v**3)))


K, K1, K2, T, S, H, S2, T3, T2, P = 1024, 512, 512, 2048, 512, 1024, 1024, 2048, 1024, 512

def setup_inputs():
    n = np.random.standard_normal
    s = mx_kscale(K)[:, None]
    u = mx_kscale(H)[:, None]
    tab_words, tab_scales = pack_weight(n((K, T)) * s, "e4m3")
    tab2_words, tab2_scales = pack_weight(n((H, T3)) / np.sqrt(H) / u, "e4m3")
    w4_words, w4_scales = pack_weight(n((K1, H)) / np.sqrt(K) / s[:K1], "e2m1")
    return {
        "tab_words": tab_words, "tab_scales": tab_scales,
        "tab2_words": tab2_words, "tab2_scales": tab2_scales,
        "w4_words": w4_words, "w4_scales": w4_scales,
        "w1": (n((K2, H)) / np.sqrt(K) / s[K1:]).astype(np.float32),
        "tide": (1.3 * np.exp(0.4 * n((H, S)))).astype(np.float32),
        "gain": (np.exp(0.3 * n(H)) * u[:, 0]).astype(np.float32),
        "wgs": np.exp(0.3 * n((128, S))).astype(np.float32),
        "page0": (n((H, T2)) * u).astype(np.float32),
        "datum": (0.9 * n((H, T2)) * u).astype(np.float32),
        "chart": (0.6 * n((S2, P))).astype(np.float32),
        "offs": striped(np.random.permutation(T)[:S]),
        "offs2": striped(np.random.permutation(T3)[:S2]),
        "offs3": striped(np.random.permutation(T2)[:S]),
        "pos1": striped(np.random.permutation(T2)[:P]),
        "pos2": striped(np.random.permutation(T2)[:P]),
    }

def reference(tab_words, tab_scales, tab2_words, tab2_scales, w4_words, w4_scales, w1, tide, gain, wgs,
              page0, datum, chart, offs, offs2, offs3, pos1, pos2):
    v = unpack_weight(tab_words, tab_scales, "e4m3")[:, unstriped(offs)]
    v2 = unpack_weight(tab2_words, tab2_scales, "e4m3")[:, unstriped(offs2)]
    w4 = unpack_weight(w4_words, w4_scales, "e2m1")
    w1q = mxq(f64(w1), 0, "e4m3")
    d = w4.T @ v[:K1] + w1q.T @ v[K1:]
    h = f64(gain)[:, None] * np.tanh(f64(tide) * d)
    page = f64(page0).copy()
    page[:, unstriped(offs3)] = np.tile(f64(wgs), (H // 128, 1)) * h
    page = mxq(page + f64(datum), 0, "e4m3")
    e = v2.T @ page
    e1 = e[:, unstriped(pos1)]
    e2 = e[:, unstriped(pos2)]
    return e1 * np.tanh(e2) + f64(chart)

@@ -1,0 +1,257 @@
+from contextlib import ExitStack
+
+import concourse.mybir as mybir
+from concourse.masks import make_identity
+
+K, T, S, H, S2, T2, PAIRS = 1024, 2048, 512, 1024, 1024, 1024, 512
+FLOPS = 2 * K * H * S + 2 * H * S2 * T2
+
+F32 = mybir.dt.float32
+BF16 = mybir.dt.bfloat16
+I32 = mybir.dt.int32
+U32 = mybir.dt.uint32
+U16 = mybir.dt.uint16
+U8 = mybir.dt.uint8
+FP8X4 = mybir.dt.float8_e4m3fn_x4
+FP4X4 = mybir.dt.float4_e2m1fn_x4
+MULT = mybir.AluOpType.mult
+ADD = mybir.AluOpType.add
+TANH = mybir.ActivationFunctionType.Tanh
+COPY = mybir.ActivationFunctionType.Copy
+
+P = 128
+BANK = 512
+PASSES = 2
+ROW_TILES = H // P
+CAND_TILES = S2 // P
+HALVES = T2 // BANK
+W1_BLOCKS = ((0, 128), (128, 384), (384, 768), (768, 1024))
+
+
+def tile_list_sounding_shoal_scores_kernel(
+    tc, tab_words, tab_scales, tab2_words, tab2_scales, w4_words, w4_scales, w1, tide, gain, wgs,
+    page0, datum, chart, offs, offs2, offs3, pos1, pos2, out,
+):
+    nc = tc.nc
+    with ExitStack() as ctx:
+        keep = ctx.enter_context(tc.tile_pool(name="keep", bufs=1))
+        ring = ctx.enter_context(tc.tile_pool(name="ring", bufs=1))
+        psum = ctx.enter_context(tc.psum_pool(name="psum", bufs=1))
+
+        def load_list(name, src):
+            tile = keep.tile(list(src.shape), U16, name=name)
+            nc.sync.dma_start(tile[:], src)
+            return tile
+
+        def load_words(name, src):
+            tile = keep.tile([P, T], U32, name=name, align_bytes=64)
+            nc.sync.dma_start(tile[:].bitcast(I32), src.rearrange("p t i -> p (t i)").bitcast(I32))
+            return tile
+
+        def load_scales(name, src, clear, queue):
+            passes, rows, width = src.shape
+            tile = keep.tile([P, width], U8, name=name, align_bytes=64)
+            clear.memset(tile[:].bitcast(I32), 0)
+            for q in range(4):
+                queue.dma_start(
+                    tile[32 * q : 32 * q + 4 * passes, :].bitcast(I32),
+                    src[:, 4 * q : 4 * q + 4, :].bitcast(I32),
+                )
+            return tile
+
+        def load_rows(name, src, i, tag=None, bufs=1):
+            tile = ring.tile([P, src.shape[1]], F32, name=name, tag=tag or name, bufs=bufs)
+            nc.sync.dma_start(tile[:], src[i * P : (i + 1) * P, :])
+            return tile
+
+        def load_w1(block):
+            lo, hi = W1_BLOCKS[block]
+            tile = keep.tile([P, 4, hi - lo], F32, name="w1_raw%d" % block)
+            nc.sync.dma_start(tile[:], w1[:, lo:hi].rearrange("(p t) c -> p t c", t=4))
+            return tile
+
+        offs_t = load_list("offs_t", offs)
+        tab_w = [load_words("tab_w0", tab_words[0])]
+        tab_s = load_scales("tab_s", tab_scales, nc.gpsimd, nc.sync)
+        w4_scale = load_scales("w4_scale", w4_scales, nc.vector, nc.scalar)
+        gain_rows = keep.tile([P, P], F32)
+        nc.gpsimd.memset(gain_rows[:], 0.0)
+        nc.scalar.dma_start(gain_rows[0:ROW_TILES, :], gain.rearrange("(i p) -> i p", p=P))
+        ident = keep.tile([P, P], F32)
+        make_identity(nc, ident[:])
+
+        w1_raw = [load_w1(0)]
+        tab_w.append(load_words("tab_w1", tab_words[1]))
+        w4_code = keep.tile([P, 2 * H], U8, align_bytes=64)
+        nc.sync.dma_start(w4_code[:].bitcast(I32), w4_words[0].bitcast(I32))
+        w1_raw.append(load_w1(1))
+        tide_t = [load_rows("tide%d" % i, tide, i, "narrow", ROW_TILES) for i in range(2)]
+        wgs_t = load_rows("wgs_t", wgs, 0)
+        offs3_t = load_list("offs3_t", offs3)
+        page_t, datum_t = [], []
+        for i in range(ROW_TILES):
+            page_t.append(load_rows("page%d" % i, page0, i))
+            if i == 0:
+                w1_raw.append(load_w1(2))
+            if i + 2 < ROW_TILES:
+                tide_t.append(load_rows("tide%d" % (i + 2), tide, i + 2, "narrow", ROW_TILES))
+            datum_t.append(load_rows("datum%d" % i, datum, i, "wide", ROW_TILES))
+            if i == 1:
+                w1_raw.append(load_w1(3))
+        offs2_t = load_list("offs2_t", offs2)
+        tab2_s = load_scales("tab2_s", tab2_scales, nc.vector, nc.sync)
+        tab2_w = [load_words("tab2_w%d" % a, tab2_words[a]) for a in range(PASSES)]
+        pos2_t = load_list("pos2_t", pos2)
+        pos1_t = load_list("pos1_t", pos1)
+
+        def gather_bytes(name, dtype, window, offsets):
+            tile = keep.tile([P, 16 * offsets.shape[1]], dtype, name=name, align_bytes=64)
+            nc.vector.tensor_copy(tile[:], window[:].indirect(offsets))
+            return tile
+
+        v_w = [gather_bytes("v_w0", U32, tab_w[0], offs_t[:])]
+        v_s = gather_bytes("v_s", U8, tab_s, offs_t[:])
+        v_w.append(gather_bytes("v_w1", U32, tab_w[1], offs_t[:]))
+
+        gain_bank = psum.tile([P, BANK], F32, tag="back", bufs=2)
+        nc.tensor.transpose(gain_bank[:, 0:P], gain_rows[:], ident[:])
+        gain_col = keep.tile([P, ROW_TILES], F32)
+        nc.scalar.copy(gain_col[:], gain_bank[:, 0:ROW_TILES])
+
+        w1_q = {}
+
+        def quantize_w1(block):
+            lo, hi = W1_BLOCKS[block]
+            width = hi - lo
+            woven = keep.tile([P, width, 4], BF16, name="w1_woven%d" % block, align_bytes=64)
+            weave = nc.vector.tensor_copy if block < 2 else nc.scalar.copy
+            weave(
+                woven[:].rearrange("p (c i) t -> p c t i", i=4),
+                w1_raw[block][:].rearrange("p t (c i) -> p c t i", i=4),
+            )
+            code = keep.tile([P, width], U32, name="w1_code%d" % block, align_bytes=64)
+            scale = keep.tile([P, width], U8, name="w1_scale%d" % block, align_bytes=64)
+            nc.vector.quantize_mx(code[:].bitcast(FP8X4), scale[:], woven[:].rearrange("p c t -> p (c t)"))
+            for i in range(lo // P, hi // P):
+                cols = slice(i * P - lo, (i + 1) * P - lo)
+                w1_q[i] = (code[:, cols], scale[:, cols])
+
+        h_t = {}
+
+        def features(i):
+            for block in range(len(W1_BLOCKS)):
+                if W1_BLOCKS[block][0] == i * P:
+                    quantize_w1(block)
+            d_bank = psum.tile([P, BANK], F32, tag="proj", bufs=2)
+            nc.tensor.matmul_mx(
+                d_bank[:],
+                lhsT=w4_code[:, 2 * P * i : 2 * P * (i + 1)].bitcast(FP4X4),
+                lhsT_scale=w4_scale[:, P * i : P * (i + 1)],
+                rhs=v_w[0][:].bitcast(FP8X4), rhs_scale=v_s[:],
+                start=True, stop=False,
+            )
+            nc.tensor.matmul_mx(
+                d_bank[:],
+                lhsT=w1_q[i][0].bitcast(FP8X4), lhsT_scale=w1_q[i][1],
+                rhs=v_w[1][:].bitcast(FP8X4), rhs_scale=v_s[4:P, :],
+                start=False, stop=True,
+            )
+            h = ring.tile([P, S], F32, tag="work", bufs=4)
+            nc.vector.tensor_tensor(h[:], d_bank[:], tide_t[i][:], MULT)
+            nc.scalar.activation(h[:], h[:], TANH)
+            nc.scalar.activation(h[:], h[:], COPY, scale=gain_col[:, i : i + 1])
+            h_t[i] = h
+
+        turned = {}
+        b_q = {}
+
+        def revise(i):
+            a, quarter = divmod(i, 4)
+            banks = [psum.tile([P, 4, P], F32, name="sum_bank", tag="wide", bufs=4) for half in range(HALVES)]
+            for half in range(HALVES):
+                for c in range(4):
+                    cols = slice(BANK * half + P * c, BANK * half + P * (c + 1))
+                    nc.tensor.matmul(banks[half][:, c, :], datum_t[i][:, cols], ident[:],
+                                     start=(c == 0), stop=False, is_transpose=True)
+            nc.vector.tensor_tensor(page_t[i][:].indirect(offs3_t[:]), wgs_t[:], h_t[i][:], MULT)
+            for half in range(HALVES):
+                for c in range(4):
+                    cols = slice(BANK * half + P * c, BANK * half + P * (c + 1))
+                    nc.tensor.matmul(banks[half][:, c, :], page_t[i][:, cols], ident[:],
+                                     start=False, stop=(c == 3), is_transpose=True)
+                if quarter == 0:
+                    turned[a, half] = keep.tile([P, 4, 2, P, 2], BF16, name="turned%d%d" % (a, half))
+                nc.scalar.copy(
+                    turned[a, half][:, :, :, 32 * quarter : 32 * (quarter + 1), :],
+                    banks[half][:].rearrange("n c (q u e) -> n c u q e", u=2, e=2),
+                )
+
+        def quantize_page(a):
+            for half in range(HALVES):
+                words = turned[a, half][:].rearrange("n c u p e -> n (c u p e)").bitcast(F32)
+                woven = keep.tile([P, BANK * 4], BF16, name="b_woven%d%d" % (a, half), align_bytes=64)
+                for pair in range(2):
+                    back = psum.tile([P, 2, 2, P], F32, name="back", tag="back", bufs=2)
+                    for c in range(2):
+                        for u in range(2):
+                            first = P * (4 * pair + 2 * c + u)
+                            nc.tensor.transpose(back[:, c, u, :], words[:, first : first + P], ident[:])
+                    nc.scalar.copy(
+                        woven[:].bitcast(F32)[:, BANK * pair : BANK * (pair + 1)].rearrange(
+                            "p (c n u) -> p c n u", c=2, u=2),
+                        back[:].rearrange("p c u n -> p c n u"),
+                    )
+                code = keep.tile([P, BANK], U32, name="b_code%d%d" % (a, half), align_bytes=64)
+                scale = keep.tile([P, BANK], U8, name="b_scale%d%d" % (a, half), align_bytes=64)
+                nc.vector.quantize_mx(code[:].bitcast(FP8X4), scale[:], woven[:])
+                b_q[a, half] = (code, scale)
+
+        features(0)
+        for i in range(ROW_TILES):
+            if i + 1 < ROW_TILES:
+                features(i + 1)
+            revise(i)
+            if i % 4 == 3:
+                quantize_page(i // 4)
+
+        chart_t = [load_rows("chart%d" % m, chart, m, "narrow", ROW_TILES) for m in range(CAND_TILES)]
+
+        cand = []
+        for part in range(2):
+            piece = offs2_t[:, 32 * part : 32 * (part + 1)]
+            scale = gather_bytes("v2_s%d" % part, U8, tab2_s, piece)
+            words = [gather_bytes("v2_w%d%d" % (part, a), U32, tab2_w[a], piece) for a in range(PASSES)]
+            cand.append((words, scale))
+
+        e_t, e2_t = {}, {}
+
+        def score(m):
+            words, scale = cand[m // 4]
+            cols = slice(P * (m % 4), P * (m % 4 + 1))
+            e = ring.tile([P, T2], F32, tag="wide", bufs=ROW_TILES)
+            for half in range(HALVES):
+                e_bank = psum.tile([P, BANK], F32, tag="wide", bufs=4)
+                for a in range(PASSES):
+                    nc.tensor.matmul_mx(
+                        e_bank[:],
+                        lhsT=words[a][:, cols].bitcast(FP8X4), lhsT_scale=scale[4 * a : P, cols],
+                        rhs=b_q[a, half][0][:].bitcast(FP8X4), rhs_scale=b_q[a, half][1][:],
+                        start=(a == 0), stop=(a == PASSES - 1),
+                    )
+                nc.scalar.copy(e[:, BANK * half : BANK * (half + 1)], e_bank[:])
+            e2 = ring.tile([P, PAIRS], F32, tag="work", bufs=4)
+            nc.vector.tensor_copy(e2[:], e[:].indirect(pos2_t[:]))
+            e_t[m], e2_t[m] = e, e2
+
+        def finish(m):
+            nc.scalar.activation(e2_t[m][:], e2_t[m][:], TANH)
+            res = ring.tile([P, PAIRS], F32, tag="res", bufs=4)
+            nc.vector.tensor_tensor(res[:], e_t[m][:].indirect(pos1_t[:]), e2_t[m][:], MULT)
+            nc.vector.tensor_tensor(res[:], res[:], chart_t[m][:], ADD)
+            nc.sync.dma_start(out[P * m : P * (m + 1), :], res[:])
+
+        score(0)
+        for m in range(CAND_TILES):
+            if m + 1 < CAND_TILES:
+                score(m + 1)
+            finish(m)

@@ -73,20 +73,20 @@ def tile_list_sounding_shoal_scores_kernel(
         offs_t = load_list("offs_t", offs)
         tab_w = [load_words("tab_w0", tab_words[0])]
         tab_s = load_scales("tab_s", tab_scales, nc.gpsimd, nc.sync)
-        w4_scale = load_scales("w4_scale", w4_scales, nc.vector, nc.scalar)
+        tab_w.append(load_words("tab_w1", tab_words[1]))
+        w1_raw = [load_w1(0)]
+        w4_scale = load_scales("w4_scale", w4_scales, nc.vector, nc.sync)
         gain_rows = keep.tile([P, P], F32)
         nc.gpsimd.memset(gain_rows[:], 0.0)
-        nc.scalar.dma_start(gain_rows[0:ROW_TILES, :], gain.rearrange("(i p) -> i p", p=P))
-        ident = keep.tile([P, P], F32)
-        make_identity(nc, ident[:])
-
-        w1_raw = [load_w1(0)]
-        tab_w.append(load_words("tab_w1", tab_words[1]))
+        nc.sync.dma_start(gain_rows[0:ROW_TILES, :], gain.rearrange("(i p) -> i p", p=P))
         w4_code = keep.tile([P, 2 * H], U8, align_bytes=64)
         nc.sync.dma_start(w4_code[:].bitcast(I32), w4_words[0].bitcast(I32))
         w1_raw.append(load_w1(1))
-        tide_t = [load_rows("tide%d" % i, tide, i, "narrow", ROW_TILES) for i in range(2)]
+        ident = keep.tile([P, P], F32)
+        make_identity(nc, ident[:])
+        tide_t = [load_rows("tide0", tide, 0, "narrow", ROW_TILES)]
         wgs_t = load_rows("wgs_t", wgs, 0)
+        tide_t.append(load_rows("tide1", tide, 1, "narrow", ROW_TILES))
         offs3_t = load_list("offs3_t", offs3)
         page_t, datum_t = [], []
         for i in range(ROW_TILES):
@@ -142,6 +142,8 @@ def tile_list_sounding_shoal_scores_kernel(
             for block in range(len(W1_BLOCKS)):
                 if W1_BLOCKS[block][0] == i * P:
                     quantize_w1(block)
+            factor = ring.tile([P, S], F32, tag="factor%d" % (i % 3), align_bytes=64)
+            nc.scalar.activation(factor[:], wgs_t[:], COPY, scale=gain_col[:, i : i + 1])
             d_bank = psum.tile([P, BANK], F32, tag="proj", bufs=2)
             nc.tensor.matmul_mx(
                 d_bank[:],
@@ -159,8 +161,7 @@ def tile_list_sounding_shoal_scores_kernel(
             h = ring.tile([P, S], F32, tag="work", bufs=4)
             nc.vector.tensor_tensor(h[:], d_bank[:], tide_t[i][:], MULT)
             nc.scalar.activation(h[:], h[:], TANH)
-            nc.scalar.activation(h[:], h[:], COPY, scale=gain_col[:, i : i + 1])
-            h_t[i] = h
+            h_t[i] = (factor, h)
 
         turned = {}
         b_q = {}
@@ -173,7 +174,7 @@ def tile_list_sounding_shoal_scores_kernel(
                     cols = slice(BANK * half + P * c, BANK * half + P * (c + 1))
                     nc.tensor.matmul(banks[half][:, c, :], datum_t[i][:, cols], ident[:],
                                      start=(c == 0), stop=False, is_transpose=True)
-            nc.vector.tensor_tensor(page_t[i][:].indirect(offs3_t[:]), wgs_t[:], h_t[i][:], MULT)
+            nc.vector.tensor_tensor(page_t[i][:].indirect(offs3_t[:]), h_t[i][0][:], h_t[i][1][:], MULT)
             for half in range(HALVES):
                 for c in range(4):
                     cols = slice(BANK * half + P * c, BANK * half + P * (c + 1))
@@ -186,10 +187,12 @@ def tile_list_sounding_shoal_scores_kernel(
                     banks[half][:].rearrange("n c (q u e) -> n c u q e", u=2, e=2),
                 )
 
-        def quantize_page(a):
+        woven_t = {}
+
+        def turn_back(a):
             for half in range(HALVES):
                 words = turned[a, half][:].rearrange("n c u p e -> n (c u p e)").bitcast(F32)
-                woven = keep.tile([P, BANK * 4], BF16, name="b_woven%d%d" % (a, half), align_bytes=64)
+                woven = keep.tile([P, BANK * 4], BF16, name="b_woven", tag="woven%d%d" % (a, half), align_bytes=64)
                 for pair in range(2):
                     back = psum.tile([P, 2, 2, P], F32, name="back", tag="back", bufs=2)
                     for c in range(2):
@@ -201,10 +204,14 @@ def tile_list_sounding_shoal_scores_kernel(
                             "p (c n u) -> p c n u", c=2, u=2),
                         back[:].rearrange("p c u n -> p c n u"),
                     )
-                code = keep.tile([P, BANK], U32, name="b_code%d%d" % (a, half), align_bytes=64)
+                woven_t[a, half] = woven
+
+        def quantize_page(a, code):
+            for half in range(HALVES):
                 scale = keep.tile([P, BANK], U8, name="b_scale%d%d" % (a, half), align_bytes=64)
-                nc.vector.quantize_mx(code[:].bitcast(FP8X4), scale[:], woven[:])
-                b_q[a, half] = (code, scale)
+                cols = slice(BANK * half, BANK * (half + 1))
+                nc.vector.quantize_mx(code[:, cols].bitcast(FP8X4), scale[:], woven_t[a, half][:])
+                b_q[a, half] = (code[:, cols], scale[:])
 
         features(0)
         for i in range(ROW_TILES):
@@ -212,7 +219,10 @@ def tile_list_sounding_shoal_scores_kernel(
                 features(i + 1)
             revise(i)
             if i % 4 == 3:
-                quantize_page(i // 4)
+                turn_back(i // 4)
+        last_factor = "factor%d" % ((ROW_TILES - 1) % 3)
+        quantize_page(0, ring.tile([P, T2], U32, name="b_code0", tag=last_factor, align_bytes=64))
+        quantize_page(1, keep.tile([P, T2], U32, name="b_code1", align_bytes=64))
 
         chart_t = [load_rows("chart%d" % m, chart, m, "narrow", ROW_TILES) for m in range(CAND_TILES)]
 
@@ -220,7 +230,10 @@ def tile_list_sounding_shoal_scores_kernel(
         for part in range(2):
             piece = offs2_t[:, 32 * part : 32 * (part + 1)]
             scale = gather_bytes("v2_s%d" % part, U8, tab2_s, piece)
-            words = [gather_bytes("v2_w%d%d" % (part, a), U32, tab2_w[a], piece) for a in range(PASSES)]
+            tag = "woven11" if part == 1 else "v2_first"
+            words = keep.tile([P, PASSES, BANK], U32, name="v2_w", tag=tag, align_bytes=64)
+            for a in range(PASSES):
+                nc.vector.tensor_copy(words[:, a, :], tab2_w[a][:].indirect(piece))
             cand.append((words, scale))
 
         e_t, e2_t = {}, {}
@@ -234,8 +247,8 @@ def tile_list_sounding_shoal_scores_kernel(
                 for a in range(PASSES):
                     nc.tensor.matmul_mx(
                         e_bank[:],
-                        lhsT=words[a][:, cols].bitcast(FP8X4), lhsT_scale=scale[4 * a : P, cols],
-                        rhs=b_q[a, half][0][:].bitcast(FP8X4), rhs_scale=b_q[a, half][1][:],
+                        lhsT=words[:, a, cols].bitcast(FP8X4), lhsT_scale=scale[4 * a : P, cols],
+                        rhs=b_q[a, half][0].bitcast(FP8X4), rhs_scale=b_q[a, half][1],
                         start=(a == 0), stop=(a == PASSES - 1),
                     )
                 nc.scalar.copy(e[:, BANK * half : BANK * (half + 1)], e_bank[:])
@@ -247,7 +260,8 @@ def tile_list_sounding_shoal_scores_kernel(
             nc.scalar.activation(e2_t[m][:], e2_t[m][:], TANH)
             res = ring.tile([P, PAIRS], F32, tag="res", bufs=4)
             nc.vector.tensor_tensor(res[:], e_t[m][:].indirect(pos1_t[:]), e2_t[m][:], MULT)
-            nc.vector.tensor_tensor(res[:], res[:], chart_t[m][:], ADD)
+            adder = nc.gpsimd if m + 1 < CAND_TILES else nc.vector
+            adder.tensor_tensor(res[:], res[:], chart_t[m][:], ADD)
             nc.sync.dma_start(out[P * m : P * (m + 1), :], res[:])
 
         score(0)

@@ -25,7 +25,7 @@ PASSES = 2
 ROW_TILES = H // P
 CAND_TILES = S2 // P
 HALVES = T2 // BANK
-W1_BLOCKS = ((0, 128), (128, 384), (384, 768), (768, 1024))
+W1_BLOCKS = ((0, 128), (128, 512), (512, 1024))
 
 
 def tile_list_sounding_shoal_scores_kernel(
@@ -73,19 +73,19 @@ def tile_list_sounding_shoal_scores_kernel(
         offs_t = load_list("offs_t", offs)
         tab_w = [load_words("tab_w0", tab_words[0])]
         tab_s = load_scales("tab_s", tab_scales, nc.gpsimd, nc.sync)
-        tab_w.append(load_words("tab_w1", tab_words[1]))
-        w1_raw = [load_w1(0)]
-        w4_scale = load_scales("w4_scale", w4_scales, nc.vector, nc.sync)
         gain_rows = keep.tile([P, P], F32)
         nc.gpsimd.memset(gain_rows[:], 0.0)
         nc.sync.dma_start(gain_rows[0:ROW_TILES, :], gain.rearrange("(i p) -> i p", p=P))
+        tab_w.append(load_words("tab_w1", tab_words[1]))
+        w1_raw = [load_w1(0)]
+        wgs_t = load_rows("wgs_t", wgs, 0)
+        w4_scale = load_scales("w4_scale", w4_scales, nc.vector, nc.sync)
         w4_code = keep.tile([P, 2 * H], U8, align_bytes=64)
         nc.sync.dma_start(w4_code[:].bitcast(I32), w4_words[0].bitcast(I32))
         w1_raw.append(load_w1(1))
         ident = keep.tile([P, P], F32)
         make_identity(nc, ident[:])
         tide_t = [load_rows("tide0", tide, 0, "narrow", ROW_TILES)]
-        wgs_t = load_rows("wgs_t", wgs, 0)
         tide_t.append(load_rows("tide1", tide, 1, "narrow", ROW_TILES))
         offs3_t = load_list("offs3_t", offs3)
         page_t, datum_t = [], []
@@ -96,8 +96,6 @@ def tile_list_sounding_shoal_scores_kernel(
             if i + 2 < ROW_TILES:
                 tide_t.append(load_rows("tide%d" % (i + 2), tide, i + 2, "narrow", ROW_TILES))
             datum_t.append(load_rows("datum%d" % i, datum, i, "wide", ROW_TILES))
-            if i == 1:
-                w1_raw.append(load_w1(3))
         offs2_t = load_list("offs2_t", offs2)
         tab2_s = load_scales("tab2_s", tab2_scales, nc.vector, nc.sync)
         tab2_w = [load_words("tab2_w%d" % a, tab2_words[a]) for a in range(PASSES)]
@@ -125,10 +123,12 @@ def tile_list_sounding_shoal_scores_kernel(
             width = hi - lo
             woven = keep.tile([P, width, 4], BF16, name="w1_woven%d" % block, align_bytes=64)
             weave = nc.vector.tensor_copy if block < 2 else nc.scalar.copy
-            weave(
-                woven[:].rearrange("p (c i) t -> p c t i", i=4),
-                w1_raw[block][:].rearrange("p t (c i) -> p c t i", i=4),
-            )
+            piece = width if block < 2 else width // 2
+            for c0 in range(0, width, piece):
+                weave(
+                    woven[:, c0 : c0 + piece, :].rearrange("p (c i) t -> p c t i", i=4),
+                    w1_raw[block][:, :, c0 : c0 + piece].rearrange("p t (c i) -> p c t i", i=4),
+                )
             code = keep.tile([P, width], U32, name="w1_code%d" % block, align_bytes=64)
             scale = keep.tile([P, width], U8, name="w1_scale%d" % block, align_bytes=64)
             nc.vector.quantize_mx(code[:].bitcast(FP8X4), scale[:], woven[:].rearrange("p c t -> p (c t)"))
@@ -142,7 +142,7 @@ def tile_list_sounding_shoal_scores_kernel(
             for block in range(len(W1_BLOCKS)):
                 if W1_BLOCKS[block][0] == i * P:
                     quantize_w1(block)
-            factor = ring.tile([P, S], F32, tag="factor%d" % (i % 3), align_bytes=64)
+            factor = ring.tile([P, S], F32, tag="factor%d" % i, align_bytes=64)
             nc.scalar.activation(factor[:], wgs_t[:], COPY, scale=gain_col[:, i : i + 1])
             d_bank = psum.tile([P, BANK], F32, tag="proj", bufs=2)
             nc.tensor.matmul_mx(
@@ -159,7 +159,11 @@ def tile_list_sounding_shoal_scores_kernel(
                 start=False, stop=True,
             )
             h = ring.tile([P, S], F32, tag="work", bufs=4)
-            nc.vector.tensor_tensor(h[:], d_bank[:], tide_t[i][:], MULT)
+            if i < 2:
+                nc.vector.tensor_tensor(h[:], d_bank[:], tide_t[i][:], MULT)
+            else:
+                nc.scalar.copy(h[:], d_bank[:])
+                nc.gpsimd.tensor_tensor(h[:], h[:], tide_t[i][:], MULT)
             nc.scalar.activation(h[:], h[:], TANH)
             h_t[i] = (factor, h)
 
@@ -174,7 +178,10 @@ def tile_list_sounding_shoal_scores_kernel(
                     cols = slice(BANK * half + P * c, BANK * half + P * (c + 1))
                     nc.tensor.matmul(banks[half][:, c, :], datum_t[i][:, cols], ident[:],
                                      start=(c == 0), stop=False, is_transpose=True)
-            nc.vector.tensor_tensor(page_t[i][:].indirect(offs3_t[:]), h_t[i][0][:], h_t[i][1][:], MULT)
+            factor, h = h_t[i]
+            engine = nc.vector if i == 0 else nc.gpsimd
+            engine.tensor_tensor(factor[:], factor[:], h[:], MULT)
+            nc.vector.tensor_copy(page_t[i][:].indirect(offs3_t[:]), factor[:])
             for half in range(HALVES):
                 for c in range(4):
                     cols = slice(BANK * half + P * c, BANK * half + P * (c + 1))
@@ -220,7 +227,7 @@ def tile_list_sounding_shoal_scores_kernel(
             revise(i)
             if i % 4 == 3:
                 turn_back(i // 4)
-        last_factor = "factor%d" % ((ROW_TILES - 1) % 3)
+        last_factor = "factor%d" % (ROW_TILES - 1)
         quantize_page(0, ring.tile([P, T2], U32, name="b_code0", tag=last_factor, align_bytes=64))
         quantize_page(1, keep.tile([P, T2], U32, name="b_code1", align_bytes=64))
 

@@ -201,7 +201,8 @@ def tile_list_sounding_shoal_scores_kernel(
                 words = turned[a, half][:].rearrange("n c u p e -> n (c u p e)").bitcast(F32)
                 woven = keep.tile([P, BANK * 4], BF16, name="b_woven", tag="woven%d%d" % (a, half), align_bytes=64)
                 for pair in range(2):
-                    back = psum.tile([P, 2, 2, P], F32, name="back", tag="back", bufs=2)
+                    tag = "proj" if (a, half) == (1, 1) else "back"
+                    back = psum.tile([P, 2, 2, P], F32, name="back", tag=tag, bufs=2)
                     for c in range(2):
                         for u in range(2):
                             first = P * (4 * pair + 2 * c + u)
@@ -263,12 +264,33 @@ def tile_list_sounding_shoal_scores_kernel(
             nc.vector.tensor_copy(e2[:], e[:].indirect(pos2_t[:]))
             e_t[m], e2_t[m] = e, e2
 
+        def add_by_transposes(res, term, spare_tag):
+            there = psum.tile([P, 4, P], F32, name="there", tag="proj", bufs=2)
+            for n, tile in enumerate((term, res)):
+                for c in range(4):
+                    nc.tensor.matmul(there[:, c, :], tile[:, P * c : P * (c + 1)], ident[:],
+                                     start=(n == 0 and c == 0), stop=(n == 1 and c == 3), is_transpose=True)
+            total = ring.tile([P, 4, P], F32, tag=spare_tag, align_bytes=64)
+            nc.scalar.copy(total[:], there[:])
+            back = psum.tile([P, 4, P], F32, name="back", tag="back", bufs=2)
+            for c in range(4):
+                nc.tensor.transpose(back[:, c, :], total[:, c, :], ident[:])
+            nc.scalar.copy(res[:], back[:].rearrange("p c n -> p (c n)"))
+
         def finish(m):
             nc.scalar.activation(e2_t[m][:], e2_t[m][:], TANH)
-            res = ring.tile([P, PAIRS], F32, tag="res", bufs=4)
-            nc.vector.tensor_tensor(res[:], e_t[m][:].indirect(pos1_t[:]), e2_t[m][:], MULT)
-            adder = nc.gpsimd if m + 1 < CAND_TILES else nc.vector
-            adder.tensor_tensor(res[:], res[:], chart_t[m][:], ADD)
+            res = ring.tile([P, PAIRS], F32, tag="res", bufs=5)
+            e1 = e_t[m][:].indirect(pos1_t[:])
+            if m + 2 >= CAND_TILES:
+                nc.vector.tensor_tensor(res[:], e1, e2_t[m][:], MULT)
+                nc.vector.tensor_tensor(res[:], res[:], chart_t[m][:], ADD)
+            else:
+                nc.vector.tensor_copy(res[:], e1)
+                nc.gpsimd.tensor_tensor(res[:], res[:], e2_t[m][:], MULT)
+                if m % 2 == 1:
+                    add_by_transposes(res, chart_t[m], "factor%d" % m)
+                else:
+                    nc.gpsimd.tensor_tensor(res[:], res[:], chart_t[m][:], ADD)
             nc.sync.dma_start(out[P * m : P * (m + 1), :], res[:])
 
         score(0)

from contextlib import ExitStack

import concourse.mybir as mybir
from concourse.masks import make_identity

K, T, S, H, S2, T2, PAIRS = 1024, 2048, 512, 1024, 1024, 1024, 512
FLOPS = 2 * K * H * S + 2 * H * S2 * T2

F32 = mybir.dt.float32
BF16 = mybir.dt.bfloat16
I32 = mybir.dt.int32
U32 = mybir.dt.uint32
U16 = mybir.dt.uint16
U8 = mybir.dt.uint8
FP8X4 = mybir.dt.float8_e4m3fn_x4
FP4X4 = mybir.dt.float4_e2m1fn_x4
MULT = mybir.AluOpType.mult
ADD = mybir.AluOpType.add
TANH = mybir.ActivationFunctionType.Tanh
COPY = mybir.ActivationFunctionType.Copy

P = 128
BANK = 512
PASSES = 2
ROW_TILES = H // P
CAND_TILES = S2 // P
HALVES = T2 // BANK
W1_BLOCKS = ((0, 128), (128, 512), (512, 1024))


def tile_list_sounding_shoal_scores_kernel(
    tc, tab_words, tab_scales, tab2_words, tab2_scales, w4_words, w4_scales, w1, tide, gain, wgs,
    page0, datum, chart, offs, offs2, offs3, pos1, pos2, out,
):
    nc = tc.nc
    with ExitStack() as ctx:
        keep = ctx.enter_context(tc.tile_pool(name="keep", bufs=1))
        ring = ctx.enter_context(tc.tile_pool(name="ring", bufs=1))
        psum = ctx.enter_context(tc.psum_pool(name="psum", bufs=1))

        def load_list(name, src):
            tile = keep.tile(list(src.shape), U16, name=name)
            nc.sync.dma_start(tile[:], src)
            return tile

        def load_words(name, src):
            tile = keep.tile([P, T], U32, name=name, align_bytes=64)
            nc.sync.dma_start(tile[:].bitcast(I32), src.rearrange("p t i -> p (t i)").bitcast(I32))
            return tile

        def load_scales(name, src, clear, queue):
            passes, rows, width = src.shape
            tile = keep.tile([P, width], U8, name=name, align_bytes=64)
            clear.memset(tile[:].bitcast(I32), 0)
            for q in range(4):
                queue.dma_start(
                    tile[32 * q : 32 * q + 4 * passes, :].bitcast(I32),
                    src[:, 4 * q : 4 * q + 4, :].bitcast(I32),
                )
            return tile

        def load_rows(name, src, i, tag=None, bufs=1):
            tile = ring.tile([P, src.shape[1]], F32, name=name, tag=tag or name, bufs=bufs)
            nc.sync.dma_start(tile[:], src[i * P : (i + 1) * P, :])
            return tile

        def load_w1(block):
            lo, hi = W1_BLOCKS[block]
            tile = keep.tile([P, 4, hi - lo], F32, name="w1_raw%d" % block)
            nc.sync.dma_start(tile[:], w1[:, lo:hi].rearrange("(p t) c -> p t c", t=4))
            return tile

        offs_t = load_list("offs_t", offs)
        tab_w = [load_words("tab_w0", tab_words[0])]
        tab_s = load_scales("tab_s", tab_scales, nc.gpsimd, nc.sync)
        gain_rows = keep.tile([P, P], F32)
        nc.gpsimd.memset(gain_rows[:], 0.0)
        nc.sync.dma_start(gain_rows[0:ROW_TILES, :], gain.rearrange("(i p) -> i p", p=P))
        tab_w.append(load_words("tab_w1", tab_words[1]))
        w1_raw = [load_w1(0)]
        wgs_t = load_rows("wgs_t", wgs, 0)
        w4_scale = load_scales("w4_scale", w4_scales, nc.vector, nc.sync)
        w4_code = keep.tile([P, 2 * H], U8, align_bytes=64)
        nc.sync.dma_start(w4_code[:].bitcast(I32), w4_words[0].bitcast(I32))
        w1_raw.append(load_w1(1))
        ident = keep.tile([P, P], F32)
        make_identity(nc, ident[:])
        tide_t = [load_rows("tide0", tide, 0, "narrow", ROW_TILES)]
        tide_t.append(load_rows("tide1", tide, 1, "narrow", ROW_TILES))
        offs3_t = load_list("offs3_t", offs3)
        page_t, datum_t = [], []
        for i in range(ROW_TILES):
            page_t.append(load_rows("page%d" % i, page0, i))
            if i == 0:
                w1_raw.append(load_w1(2))
            if i + 2 < ROW_TILES:
                tide_t.append(load_rows("tide%d" % (i + 2), tide, i + 2, "narrow", ROW_TILES))
            datum_t.append(load_rows("datum%d" % i, datum, i, "wide", ROW_TILES))
        offs2_t = load_list("offs2_t", offs2)
        tab2_s = load_scales("tab2_s", tab2_scales, nc.vector, nc.sync)
        tab2_w = [load_words("tab2_w%d" % a, tab2_words[a]) for a in range(PASSES)]
        pos2_t = load_list("pos2_t", pos2)
        pos1_t = load_list("pos1_t", pos1)

        def gather_bytes(name, dtype, window, offsets):
            tile = keep.tile([P, 16 * offsets.shape[1]], dtype, name=name, align_bytes=64)
            nc.vector.tensor_copy(tile[:], window[:].indirect(offsets))
            return tile

        v_w = [gather_bytes("v_w0", U32, tab_w[0], offs_t[:])]
        v_s = gather_bytes("v_s", U8, tab_s, offs_t[:])
        v_w.append(gather_bytes("v_w1", U32, tab_w[1], offs_t[:]))

        gain_bank = psum.tile([P, BANK], F32, tag="back", bufs=2)
        nc.tensor.transpose(gain_bank[:, 0:P], gain_rows[:], ident[:])
        gain_col = keep.tile([P, ROW_TILES], F32)
        nc.scalar.copy(gain_col[:], gain_bank[:, 0:ROW_TILES])

        w1_q = {}

        def quantize_w1(block):
            lo, hi = W1_BLOCKS[block]
            width = hi - lo
            woven = keep.tile([P, width, 4], BF16, name="w1_woven%d" % block, align_bytes=64)
            weave = nc.vector.tensor_copy if block < 2 else nc.scalar.copy
            piece = width if block < 2 else width // 2
            for c0 in range(0, width, piece):
                weave(
                    woven[:, c0 : c0 + piece, :].rearrange("p (c i) t -> p c t i", i=4),
                    w1_raw[block][:, :, c0 : c0 + piece].rearrange("p t (c i) -> p c t i", i=4),
                )
            code = keep.tile([P, width], U32, name="w1_code%d" % block, align_bytes=64)
            scale = keep.tile([P, width], U8, name="w1_scale%d" % block, align_bytes=64)
            nc.vector.quantize_mx(code[:].bitcast(FP8X4), scale[:], woven[:].rearrange("p c t -> p (c t)"))
            for i in range(lo // P, hi // P):
                cols = slice(i * P - lo, (i + 1) * P - lo)
                w1_q[i] = (code[:, cols], scale[:, cols])

        h_t = {}

        def features(i):
            for block in range(len(W1_BLOCKS)):
                if W1_BLOCKS[block][0] == i * P:
                    quantize_w1(block)
            factor = ring.tile([P, S], F32, tag="factor%d" % i, align_bytes=64)
            nc.scalar.activation(factor[:], wgs_t[:], COPY, scale=gain_col[:, i : i + 1])
            d_bank = psum.tile([P, BANK], F32, tag="proj", bufs=2)
            nc.tensor.matmul_mx(
                d_bank[:],
                lhsT=w4_code[:, 2 * P * i : 2 * P * (i + 1)].bitcast(FP4X4),
                lhsT_scale=w4_scale[:, P * i : P * (i + 1)],
                rhs=v_w[0][:].bitcast(FP8X4), rhs_scale=v_s[:],
                start=True, stop=False,
            )
            nc.tensor.matmul_mx(
                d_bank[:],
                lhsT=w1_q[i][0].bitcast(FP8X4), lhsT_scale=w1_q[i][1],
                rhs=v_w[1][:].bitcast(FP8X4), rhs_scale=v_s[4:P, :],
                start=False, stop=True,
            )
            h = ring.tile([P, S], F32, tag="work", bufs=4)
            if i < 2:
                nc.vector.tensor_tensor(h[:], d_bank[:], tide_t[i][:], MULT)
            else:
                nc.scalar.copy(h[:], d_bank[:])
                nc.gpsimd.tensor_tensor(h[:], h[:], tide_t[i][:], MULT)
            nc.scalar.activation(h[:], h[:], TANH)
            h_t[i] = (factor, h)

        turned = {}
        b_q = {}

        def revise(i):
            a, quarter = divmod(i, 4)
            banks = [psum.tile([P, 4, P], F32, name="sum_bank", tag="wide", bufs=4) for half in range(HALVES)]
            for half in range(HALVES):
                for c in range(4):
                    cols = slice(BANK * half + P * c, BANK * half + P * (c + 1))
                    nc.tensor.matmul(banks[half][:, c, :], datum_t[i][:, cols], ident[:],
                                     start=(c == 0), stop=False, is_transpose=True)
            factor, h = h_t[i]
            engine = nc.vector if i == 0 else nc.gpsimd
            engine.tensor_tensor(factor[:], factor[:], h[:], MULT)
            nc.vector.tensor_copy(page_t[i][:].indirect(offs3_t[:]), factor[:])
            for half in range(HALVES):
                for c in range(4):
                    cols = slice(BANK * half + P * c, BANK * half + P * (c + 1))
                    nc.tensor.matmul(banks[half][:, c, :], page_t[i][:, cols], ident[:],
                                     start=False, stop=(c == 3), is_transpose=True)
                if quarter == 0:
                    turned[a, half] = keep.tile([P, 4, 2, P, 2], BF16, name="turned%d%d" % (a, half))
                nc.scalar.copy(
                    turned[a, half][:, :, :, 32 * quarter : 32 * (quarter + 1), :],
                    banks[half][:].rearrange("n c (q u e) -> n c u q e", u=2, e=2),
                )

        woven_t = {}

        def turn_back(a):
            for half in range(HALVES):
                words = turned[a, half][:].rearrange("n c u p e -> n (c u p e)").bitcast(F32)
                woven = keep.tile([P, BANK * 4], BF16, name="b_woven", tag="woven%d%d" % (a, half), align_bytes=64)
                for pair in range(2):
                    tag = "proj" if (a, half) == (1, 1) else "back"
                    back = psum.tile([P, 2, 2, P], F32, name="back", tag=tag, bufs=2)
                    for c in range(2):
                        for u in range(2):
                            first = P * (4 * pair + 2 * c + u)
                            nc.tensor.transpose(back[:, c, u, :], words[:, first : first + P], ident[:])
                    nc.scalar.copy(
                        woven[:].bitcast(F32)[:, BANK * pair : BANK * (pair + 1)].rearrange(
                            "p (c n u) -> p c n u", c=2, u=2),
                        back[:].rearrange("p c u n -> p c n u"),
                    )
                woven_t[a, half] = woven

        def quantize_page(a, code):
            for half in range(HALVES):
                scale = keep.tile([P, BANK], U8, name="b_scale%d%d" % (a, half), align_bytes=64)
                cols = slice(BANK * half, BANK * (half + 1))
                nc.vector.quantize_mx(code[:, cols].bitcast(FP8X4), scale[:], woven_t[a, half][:])
                b_q[a, half] = (code[:, cols], scale[:])

        features(0)
        for i in range(ROW_TILES):
            if i + 1 < ROW_TILES:
                features(i + 1)
            revise(i)
            if i % 4 == 3:
                turn_back(i // 4)
        last_factor = "factor%d" % (ROW_TILES - 1)
        quantize_page(0, ring.tile([P, T2], U32, name="b_code0", tag=last_factor, align_bytes=64))
        quantize_page(1, keep.tile([P, T2], U32, name="b_code1", align_bytes=64))

        chart_t = [load_rows("chart%d" % m, chart, m, "narrow", ROW_TILES) for m in range(CAND_TILES)]

        cand = []
        for part in range(2):
            piece = offs2_t[:, 32 * part : 32 * (part + 1)]
            scale = gather_bytes("v2_s%d" % part, U8, tab2_s, piece)
            tag = "woven11" if part == 1 else "v2_first"
            words = keep.tile([P, PASSES, BANK], U32, name="v2_w", tag=tag, align_bytes=64)
            for a in range(PASSES):
                nc.vector.tensor_copy(words[:, a, :], tab2_w[a][:].indirect(piece))
            cand.append((words, scale))

        e_t, e2_t = {}, {}

        def score(m):
            words, scale = cand[m // 4]
            cols = slice(P * (m % 4), P * (m % 4 + 1))
            e = ring.tile([P, T2], F32, tag="wide", bufs=ROW_TILES)
            for half in range(HALVES):
                e_bank = psum.tile([P, BANK], F32, tag="wide", bufs=4)
                for a in range(PASSES):
                    nc.tensor.matmul_mx(
                        e_bank[:],
                        lhsT=words[:, a, cols].bitcast(FP8X4), lhsT_scale=scale[4 * a : P, cols],
                        rhs=b_q[a, half][0].bitcast(FP8X4), rhs_scale=b_q[a, half][1],
                        start=(a == 0), stop=(a == PASSES - 1),
                    )
                nc.scalar.copy(e[:, BANK * half : BANK * (half + 1)], e_bank[:])
            e2 = ring.tile([P, PAIRS], F32, tag="work", bufs=4)
            nc.vector.tensor_copy(e2[:], e[:].indirect(pos2_t[:]))
            e_t[m], e2_t[m] = e, e2

        def add_by_transposes(res, term, spare_tag):
            there = psum.tile([P, 4, P], F32, name="there", tag="proj", bufs=2)
            for n, tile in enumerate((term, res)):
                for c in range(4):
                    nc.tensor.matmul(there[:, c, :], tile[:, P * c : P * (c + 1)], ident[:],
                                     start=(n == 0 and c == 0), stop=(n == 1 and c == 3), is_transpose=True)
            total = ring.tile([P, 4, P], F32, tag=spare_tag, align_bytes=64)
            nc.scalar.copy(total[:], there[:])
            back = psum.tile([P, 4, P], F32, name="back", tag="back", bufs=2)
            for c in range(4):
                nc.tensor.transpose(back[:, c, :], total[:, c, :], ident[:])
            nc.scalar.copy(res[:], back[:].rearrange("p c n -> p (c n)"))

        def finish(m):
            nc.scalar.activation(e2_t[m][:], e2_t[m][:], TANH)
            res = ring.tile([P, PAIRS], F32, tag="res", bufs=5)
            e1 = e_t[m][:].indirect(pos1_t[:])
            if m + 2 >= CAND_TILES:
                nc.vector.tensor_tensor(res[:], e1, e2_t[m][:], MULT)
                nc.vector.tensor_tensor(res[:], res[:], chart_t[m][:], ADD)
            else:
                nc.vector.tensor_copy(res[:], e1)
                nc.gpsimd.tensor_tensor(res[:], res[:], e2_t[m][:], MULT)
                if m % 2 == 1:
                    add_by_transposes(res, chart_t[m], "factor%d" % m)
                else:
                    nc.gpsimd.tensor_tensor(res[:], res[:], chart_t[m][:], ADD)
            nc.sync.dma_start(out[P * m : P * (m + 1), :], res[:])

        score(0)
        for m in range(CAND_TILES):
            if m + 1 < CAND_TILES:
                score(m + 1)
            finish(m)
